import numpy as np
import ml_dtypes


def mxq(x, axis, fmt="e4m3"):
    dtype, down = {"e4m3": (ml_dtypes.float8_e4m3fn, 7), "e5m2": (ml_dtypes.float8_e5m2, 14)}[fmt]
    v = np.moveaxis(np.asarray(x, np.float32).astype(ml_dtypes.bfloat16).astype(np.float64), axis, -1)
    blocks = v.reshape(v.shape[:-1] + (-1, 32))
    amax = np.abs(blocks).max(-1, keepdims=True)
    byte = np.maximum(np.where(amax > 0, np.frexp(amax)[1] - 1 + 127, 0) - down, 1)
    scale = np.exp2(byte - 127.0)
    codes = (blocks / scale).astype(np.float32).astype(dtype).astype(np.float64)
    return np.moveaxis((codes * scale).reshape(v.shape), -1, axis)


WIDE = False


def mx_kscale(k):
    if not WIDE:
        return np.ones(k)
    levels = np.array([10, -10, 5, -5, 0])
    if k % 512:
        return np.exp2(np.random.permutation(np.resize(levels, k // 32))).repeat(32)
    a = np.empty((k // 512, 16))
    for p in range(k // 512):
        a[p, :8] = np.random.permutation(np.resize(levels, 8))
        for g in range(8):
            far = levels[np.abs(levels - a[p, g]) >= 10]
            a[p, g + 8] = far[np.random.randint(len(far))]
    return np.exp2(a.ravel()).repeat(32)


def f64(x):
    return np.asarray(x).astype(np.float64)


def striped(idx):
    return np.tile(np.asarray(idx).reshape(-1, 16).T, (8, 1)).astype(np.uint16)


def unstriped(offs):
    return offs[:16].T.reshape(-1).astype(np.int64)


E2M1 = np.array([0.0, 0.5, 1.0, 1.5, 2.0, 3.0, 4.0, 6.0, -0.0, -0.5, -1.0, -1.5, -2.0, -3.0, -4.0, -6.0])


def pack_weight(w, fmt):
    k, n = w.shape
    w = f64(np.asarray(w, np.float32).astype(ml_dtypes.bfloat16)).reshape(k // 32, 32, n)
    amax = np.abs(w).max(1)
    if fmt == "e4m3":
        byte = np.frexp(amax)[1] - 1 + 127 - 7
    else:
        mant, ex = np.frexp(amax / 6.0)
        byte = np.where(mant > 0.5, ex, ex - 1) + 127
    byte = np.clip(np.where(amax > 0, byte, 1), 1, 254)
    scaled = (w * np.exp2(127.0 - byte)[:, None, :]).reshape(k, n).astype(np.float32)
    by_word = np.ascontiguousarray(scaled.reshape(k // 512, 128, 4, n).transpose(0, 1, 3, 2))
    if fmt == "e4m3":
        words = by_word.astype(ml_dtypes.float8_e4m3fn).view(np.uint8)
    else:
        c = by_word.astype(ml_dtypes.float4_e2m1fn).view(np.uint8) & 0xF
        words = (c[..., 0::2] | (c[..., 1::2] << 4)).reshape(k // 512, 128, 2 * n)
    return np.ascontiguousarray(words), np.ascontiguousarray(byte.astype(np.uint8).reshape(k // 512, 16, n))


def unpack_weight(words, scales, fmt):
    g, _, n = scales.shape
    words = np.ascontiguousarray(words).reshape(g, 128, n, -1)
    if fmt == "e4m3":
        vals = words.view(ml_dtypes.float8_e4m3fn).astype(np.float64)
    else:
        nib = np.empty((g, 128, n, 4), np.uint8)
        nib[..., 0::2] = words & 0xF
        nib[..., 1::2] = words >> 4
        vals = E2M1[nib]
    vals = vals * np.repeat(np.exp2(scales.astype(np.float64) - 127.0), 8, axis=1)[..., None]
    return vals.transpose(0, 1, 3, 2).reshape(g * 512, n)


D, E, T, I, Q, G = 512, 512, 2048, 512, 128, 64


def setup_inputs():
    n = np.random.standard_normal
    idx = np.random.permutation(T)[:I]
    fd = mx_kscale(D)
    fe = mx_kscale(E)
    keysp = pack_weight(n((D, T)) / fd[:, None], "e2m1")
    valsp = pack_weight(n((E, T)) / fe[:, None], "e2m1")
    return {
        "query": (n((D, Q)) * 0.6 / np.sqrt(D) * fd[:, None]).astype(np.float32),
        "keys_words": keysp[0],
        "keys_scales": keysp[1],
        "pw": (np.random.uniform(0.5, 1.6, (Q, 1))).astype(np.float32),
        "gout": (n((E, Q)) * 1 / np.sqrt(E) * fe[:, None]).astype(np.float32),
        "vals_words": valsp[0],
        "vals_scales": valsp[1],
        "old": (0.5 * n((Q, T))).astype(np.float32),
        "offs": striped(idx),
    }


def reference(query, keys_words, keys_scales, pw, gout, vals_words, vals_scales, old, offs):
    idx = unstriped(offs)
    keysu = unpack_weight(keys_words, keys_scales, "e2m1")
    valsu = unpack_weight(vals_words, vals_scales, "e2m1")
    queryq = mxq(f64(query), 0, "e4m3")
    keysidxg = keysu[:, idx]
    a = queryq.T @ keysidxg
    x1 = np.exp(a)
    s = x1.reshape(Q, G, I // G).sum(axis=2)
    z = np.sum(x1, axis=1, keepdims=True)
    ls = np.log(s)
    lr = np.repeat(ls, I // G, axis=1)
    sr = np.repeat(s, I // G, axis=1)
    goutq = mxq(f64(gout), 0, "e4m3")
    valsidxg = valsu[:, idx]
    c0 = goutq.T @ valsidxg
    dsr = c0 / z * np.exp((a - lr) * f64(pw))
    dlr = c0 / z * sr * np.exp((a - lr) * f64(pw)) * f64(pw) * (-1.0)
    dls = dlr.reshape(Q, G, I // G).sum(axis=2)
    dz = np.sum(c0 * np.exp((a - lr) * f64(pw)) * sr / np.square(z) * (-1.0), axis=1, keepdims=True)
    ds = dsr.reshape(Q, G, I // G).sum(axis=2) + dls / s
    r1 = np.repeat(ds, I // G, axis=1)
    dx1 = dz + r1
    da = c0 / z * sr * np.exp((a - lr) * f64(pw)) * f64(pw) + dx1 * x1
    gs = da * 128.0
    gf = np.zeros((Q, T))
    gf[:, idx] = gs
    y = f64(old) + gf
    return y

@@ -1,0 +1,164 @@
+from contextlib import ExitStack
+
+import concourse.mybir as mybir
+
+D, E, T, I, Q, G = 512, 512, 2048, 512, 128, 64
+PAGE = I // G
+P = 128
+PACK = 4
+FLOPS = 2 * Q * I * (D + E)
+
+F32 = mybir.dt.float32
+BF16 = mybir.dt.bfloat16
+I32 = mybir.dt.int32
+U32 = mybir.dt.uint32
+U16 = mybir.dt.uint16
+U8 = mybir.dt.uint8
+FP8X4 = mybir.dt.float8_e4m3fn_x4
+FP4X4 = mybir.dt.float4_e2m1fn_x4
+ALU = mybir.AluOpType
+ACT = mybir.ActivationFunctionType
+AX = mybir.AxisListType
+
+OUT_CHUNK = 512
+LN_FLOOR = 2.0 ** -62
+
+
+def tile_attend_bsharedpower_s_kernel(tc, query, keys_words, keys_scales, pw, gout, vals_words, vals_scales, old, offs, out):
+    nc = tc.nc
+    with ExitStack() as ctx:
+        sb = ctx.enter_context(tc.tile_pool(name="sb", bufs=1))
+        ps = ctx.enter_context(tc.psum_pool(name="ps", bufs=1))
+
+        def tile(name, shape, dtype, tag=""):
+            return sb.tile(shape, dtype, name=name, tag=tag or name, align_bytes=64)
+
+        def paged(ap):
+            return ap.rearrange("p (g j) -> p g j", j=PAGE)
+
+        def spread(ap):
+            return ap.unsqueeze(2).to_broadcast([P, G, PAGE])
+
+        offsets = tile("offsets", [P, I // 16], U16)
+        k_words = tile("k_words", [P, T], U16)
+        v_words = tile("v_words", [P, T], U16)
+        k_scales = tile("k_scales", [P, T], U8)
+        v_scales = tile("v_scales", [P, T], U8)
+        q_raw = tile("q_raw", [P, PACK, Q], F32)
+        g_raw = tile("g_raw", [P, PACK, Q], F32)
+        power = tile("power", [P, 1], F32)
+        old_sb = tile("old_sb", [P, T], F32)
+        placed = tile("placed", [P, T], F32)
+
+        nc.vector.memset(k_scales[:].bitcast(I32), 0)
+        nc.vector.memset(v_scales[:].bitcast(I32), 0)
+        nc.vector.memset(placed[:].bitcast(I32), 0)
+
+        def load_scales(queue, dst, src):
+            for quad in range(4):
+                queue.dma_start(out=dst[32 * quad : 32 * quad + 4, :].bitcast(I32), in_=src[0, 4 * quad : 4 * quad + 4, :].bitcast(I32))
+
+        nc.sync.dma_start(offsets[:], offs)
+        nc.sync.dma_start(out=k_words[:].bitcast(I32), in_=keys_words[0].bitcast(I32))
+        load_scales(nc.scalar, k_scales, keys_scales)
+        nc.sync.dma_start(out=q_raw[:], in_=query.rearrange("(p j) w -> p j w", j=PACK))
+        nc.sync.dma_start(out=v_words[:].bitcast(I32), in_=vals_words[0].bitcast(I32))
+        nc.sync.dma_start(out=g_raw[:], in_=gout.rearrange("(p j) w -> p j w", j=PACK))
+        nc.sync.dma_start(out=power[:], in_=pw)
+        load_scales(nc.sync, v_scales, vals_scales)
+        nc.sync.dma_start(out=old_sb[:], in_=old)
+
+        def gather(name, window, dtype, tag):
+            picked = tile(name, [P, I], dtype, tag)
+            nc.vector.tensor_copy(picked[:], window[:].indirect(offsets[:]))
+            return picked
+
+        def interleave(name, raw, copy):
+            grouped = tile(name, [P, Q, PACK], BF16)
+            copy(out=grouped[:], in_=raw[:].rearrange("p j w -> p w j"))
+            return grouped
+
+        def quantize(name, grouped):
+            codes = tile(name + "_codes", [P, Q], U32)
+            scales = tile(name + "_scales", [P, Q], U8)
+            nc.vector.quantize_mx(out=codes[:].bitcast(FP8X4), scales=scales[:], in_=grouped[:].rearrange("p w j -> p (w j)"))
+            return codes, scales
+
+        def product(name, codes, scales, words, word_scales):
+            acc = ps.tile([P, I], F32, name=name)
+            nc.tensor.matmul_mx(
+                out=acc[:],
+                lhsT=codes[:].bitcast(FP8X4),
+                lhsT_scale=scales[:],
+                rhs=words[:].bitcast(FP4X4),
+                rhs_scale=word_scales[:],
+                start=True,
+                stop=True,
+            )
+            return acc
+
+        q_grouped = interleave("q_grouped", q_raw, nc.scalar.copy)
+        ks_picked = gather("ks_picked", k_scales, U8, "picked_scales")
+        kw_picked = gather("kw_picked", k_words, U16, "picked_words")
+        q_codes, q_scales = quantize("q", q_grouped)
+        score = product("score", q_codes, q_scales, kw_picked, ks_picked)
+
+        neg_power = tile("neg_power", [P, 1], F32)
+        co_power = tile("co_power", [P, 1], F32)
+        nc.gpsimd.tensor_scalar(neg_power[:], power[:], -1.0, 0.0, ALU.mult, ALU.add)
+        nc.gpsimd.tensor_scalar(co_power[:], power[:], -1.0, 1.0, ALU.mult, ALU.add)
+
+        g_grouped = interleave("g_grouped", g_raw, nc.gpsimd.tensor_copy)
+        g_codes, g_scales = quantize("g", g_grouped)
+
+        neg_max = tile("neg_max", [P, 1], F32)
+        nc.vector.tensor_reduce(neg_max[:], score[:], AX.X, ALU.max, negate=True)
+        neg_pmax = tile("neg_pmax", [P, 1], F32)
+        nc.gpsimd.tensor_scalar(neg_pmax[:], neg_max[:], power[:], 0.0, ALU.mult, ALU.add)
+        x = tile("x", [P, I], F32)
+        z = tile("z", [P, 1], F32)
+        nc.scalar.activation(x[:], score[:], ACT.Exp, bias=neg_max[:], accum_out=z[:])
+        x_pow = tile("x_pow", [P, I], F32)
+        nc.scalar.activation(x_pow[:], score[:], ACT.Exp, bias=neg_pmax[:], scale=power[:])
+
+        vw_picked = gather("vw_picked", v_words, U16, "picked_words")
+        page_sum = tile("page_sum", [P, G], F32)
+        nc.vector.tensor_reduce(page_sum[:], paged(x[:]), AX.X, ALU.add)
+        vs_picked = gather("vs_picked", v_scales, U8, "picked_scales")
+        c0 = product("c0", g_codes, g_scales, vw_picked, vs_picked)
+
+        ln_z = tile("ln_z", [P, 1], F32)
+        nc.scalar.activation(ln_z[:], z[:], ACT.Ln)
+        neg_ln_z = tile("neg_ln_z", [P, 1], F32)
+        nc.gpsimd.tensor_scalar(neg_ln_z[:], ln_z[:], -1.0, 0.0, ALU.mult, ALU.add)
+        ln_s = tile("ln_s", [P, G], F32)
+        nc.scalar.activation(ln_s[:], page_sum[:], ACT.Ln, bias=LN_FLOOR)
+        inv_z = tile("inv_z", [P, 1], F32)
+        nc.scalar.activation(inv_z[:], ln_z[:], ACT.Exp, scale=-1.0)
+        share = tile("share", [P, G], F32)
+        nc.scalar.activation(share[:], ln_s[:], ACT.Exp, bias=neg_ln_z[:], scale=co_power[:])
+        norm = tile("norm", [P, G], F32)
+        nc.scalar.activation(norm[:], ln_s[:], ACT.Exp, bias=neg_ln_z[:], scale=neg_power[:])
+
+        v = tile("v", [P, I], F32)
+        nc.vector.scalar_tensor_tensor(v[:], c0[:], 128.0, x_pow[:], ALU.mult, ALU.mult)
+        v_sum = tile("v_sum", [P, G], F32)
+        nc.vector.tensor_reduce(v_sum[:], paged(v[:]), AX.X, ALU.add)
+        row_terms = tile("row_terms", [P, G], F32)
+        row_total = tile("row_total", [P, 1], F32)
+        nc.vector.scalar_tensor_tensor(row_terms[:], v_sum[:], inv_z[:], share[:], ALU.mult, ALU.mult, accum_out=row_total[:])
+        page_terms = tile("page_terms", [P, G], F32)
+        nc.vector.scalar_tensor_tensor(page_terms[:], v_sum[:], co_power[:], norm[:], ALU.mult, ALU.mult)
+        direct = tile("direct", [P, I], F32)
+        nc.vector.scalar_tensor_tensor(paged(direct[:]), paged(v[:]), power[:], spread(share[:]), ALU.mult, ALU.mult)
+        through = tile("through", [P, I], F32)
+        nc.vector.scalar_tensor_tensor(paged(through[:]), spread(page_terms[:]), row_total[:], paged(x[:]), ALU.subtract, ALU.mult)
+
+        nc.vector.tensor_tensor(placed[:].indirect(offsets[:]), direct[:], through[:], ALU.add)
+
+        for c in range(T // OUT_CHUNK):
+            cols = slice(c * OUT_CHUNK, (c + 1) * OUT_CHUNK)
+            result = tile("result%d" % c, [P, OUT_CHUNK], F32)
+            nc.vector.tensor_tensor(result[:], placed[:, cols], old_sb[:, cols], ALU.add)
+            queue = nc.sync if c % 2 == 0 else nc.scalar
+            queue.dma_start(out=out[:, cols], in_=result[:])

@@ -20,7 +20,10 @@ ALU = mybir.AluOpType
 ACT = mybir.ActivationFunctionType
 AX = mybir.AxisListType
 
-OUT_CHUNK = 512
+HALVES = 2
+HALF = I // HALVES
+HALF_PAGES = G // HALVES
+OUT_CHUNKS = (256, 512, 512, 512, 256)
 LN_FLOOR = 2.0 ** -62
 
 
@@ -33,11 +36,17 @@ def tile_attend_bsharedpower_s_kernel(tc, query, keys_words, keys_scales, pw, go
         def tile(name, shape, dtype, tag=""):
             return sb.tile(shape, dtype, name=name, tag=tag or name, align_bytes=64)
 
+        def slots(h):
+            return slice(h * HALF, (h + 1) * HALF)
+
+        def pages(h):
+            return slice(h * HALF_PAGES, (h + 1) * HALF_PAGES)
+
         def paged(ap):
             return ap.rearrange("p (g j) -> p g j", j=PAGE)
 
-        def spread(ap):
-            return ap.unsqueeze(2).to_broadcast([P, G, PAGE])
+        def spread(ap, times):
+            return ap.unsqueeze(2).to_broadcast([P, ap.shape[1], times])
 
         offsets = tile("offsets", [P, I // 16], U16)
         k_words = tile("k_words", [P, T], U16)
@@ -50,115 +59,140 @@ def tile_attend_bsharedpower_s_kernel(tc, query, keys_words, keys_scales, pw, go
         old_sb = tile("old_sb", [P, T], F32)
         placed = tile("placed", [P, T], F32)
 
-        nc.vector.memset(k_scales[:].bitcast(I32), 0)
-        nc.vector.memset(v_scales[:].bitcast(I32), 0)
-        nc.vector.memset(placed[:].bitcast(I32), 0)
+        nc.gpsimd.memset(k_scales[:].bitcast(I32), 0)
+        nc.gpsimd.memset(v_scales[:].bitcast(I32), 0)
+        nc.gpsimd.memset(placed[:].bitcast(I32), 0)
 
-        def load_scales(queue, dst, src):
-            for quad in range(4):
+        def load_scales(queue, dst, src, quads):
+            for quad in quads:
                 queue.dma_start(out=dst[32 * quad : 32 * quad + 4, :].bitcast(I32), in_=src[0, 4 * quad : 4 * quad + 4, :].bitcast(I32))
 
         nc.sync.dma_start(offsets[:], offs)
-        nc.sync.dma_start(out=k_words[:].bitcast(I32), in_=keys_words[0].bitcast(I32))
-        load_scales(nc.scalar, k_scales, keys_scales)
         nc.sync.dma_start(out=q_raw[:], in_=query.rearrange("(p j) w -> p j w", j=PACK))
-        nc.sync.dma_start(out=v_words[:].bitcast(I32), in_=vals_words[0].bitcast(I32))
+        nc.scalar.dma_start(out=power[:], in_=pw)
+        load_scales(nc.sync, k_scales, keys_scales, (0, 1))
+        load_scales(nc.scalar, k_scales, keys_scales, (2, 3))
+        nc.sync.dma_start(out=k_words[:].bitcast(I32), in_=keys_words[0].bitcast(I32))
         nc.sync.dma_start(out=g_raw[:], in_=gout.rearrange("(p j) w -> p j w", j=PACK))
-        nc.sync.dma_start(out=power[:], in_=pw)
-        load_scales(nc.sync, v_scales, vals_scales)
+        nc.sync.dma_start(out=v_words[:].bitcast(I32), in_=vals_words[0].bitcast(I32))
+        load_scales(nc.sync, v_scales, vals_scales, range(4))
         nc.sync.dma_start(out=old_sb[:], in_=old)
 
-        def gather(name, window, dtype, tag):
-            picked = tile(name, [P, I], dtype, tag)
+        def gather_whole(picked, window):
             nc.vector.tensor_copy(picked[:], window[:].indirect(offsets[:]))
-            return picked
 
-        def interleave(name, raw, copy):
-            grouped = tile(name, [P, Q, PACK], BF16)
-            copy(out=grouped[:], in_=raw[:].rearrange("p j w -> p w j"))
-            return grouped
+        def gather_half(picked, window, h):
+            nc.vector.tensor_copy(picked[:, slots(h)], window[:].indirect(offsets[:, h * HALF // 16 : (h + 1) * HALF // 16]))
 
-        def quantize(name, grouped):
+        def quantize(name, raw):
+            grouped = tile(name + "_grouped", [P, Q, PACK], BF16)
+            nc.scalar.copy(out=grouped[:], in_=raw[:].rearrange("p j w -> p w j"))
             codes = tile(name + "_codes", [P, Q], U32)
             scales = tile(name + "_scales", [P, Q], U8)
             nc.vector.quantize_mx(out=codes[:].bitcast(FP8X4), scales=scales[:], in_=grouped[:].rearrange("p w j -> p (w j)"))
             return codes, scales
 
-        def product(name, codes, scales, words, word_scales):
-            acc = ps.tile([P, I], F32, name=name)
+        def product(name, codes, scales, words, word_scales, h):
+            acc = ps.tile([P, HALF], F32, name="%s%d" % (name, h))
             nc.tensor.matmul_mx(
                 out=acc[:],
                 lhsT=codes[:].bitcast(FP8X4),
                 lhsT_scale=scales[:],
-                rhs=words[:].bitcast(FP4X4),
-                rhs_scale=word_scales[:],
+                rhs=words[:, slots(h)].bitcast(FP4X4),
+                rhs_scale=word_scales[:, slots(h)],
                 start=True,
                 stop=True,
             )
             return acc
 
-        q_grouped = interleave("q_grouped", q_raw, nc.scalar.copy)
-        ks_picked = gather("ks_picked", k_scales, U8, "picked_scales")
-        kw_picked = gather("kw_picked", k_words, U16, "picked_words")
-        q_codes, q_scales = quantize("q", q_grouped)
-        score = product("score", q_codes, q_scales, kw_picked, ks_picked)
+        ks_picked = tile("ks_picked", [P, I], U8)
+        kw_picked = tile("kw_picked", [P, I], U16, "picked_words")
+        gather_whole(ks_picked, k_scales)
+        q_codes, q_scales = quantize("q", q_raw)
+        score = []
+        for h in range(HALVES):
+            gather_half(kw_picked, k_words, h)
+            score.append(product("score", q_codes, q_scales, kw_picked, ks_picked, h))
+        g_codes, g_scales = quantize("g", g_raw)
 
         neg_power = tile("neg_power", [P, 1], F32)
         co_power = tile("co_power", [P, 1], F32)
         nc.gpsimd.tensor_scalar(neg_power[:], power[:], -1.0, 0.0, ALU.mult, ALU.add)
         nc.gpsimd.tensor_scalar(co_power[:], power[:], -1.0, 1.0, ALU.mult, ALU.add)
 
-        g_grouped = interleave("g_grouped", g_raw, nc.gpsimd.tensor_copy)
-        g_codes, g_scales = quantize("g", g_grouped)
-
-        neg_max = tile("neg_max", [P, 1], F32)
-        nc.vector.tensor_reduce(neg_max[:], score[:], AX.X, ALU.max, negate=True)
-        neg_pmax = tile("neg_pmax", [P, 1], F32)
-        nc.gpsimd.tensor_scalar(neg_pmax[:], neg_max[:], power[:], 0.0, ALU.mult, ALU.add)
+        neg_score = tile("neg_score", [P, I], F32)
+        neg_max = tile("neg_max", [P, HALVES], F32)
+        neg_pmax = tile("neg_pmax", [P, HALVES], F32, "late_scales")
+        half_sum = tile("half_sum", [P, HALVES], F32)
         x = tile("x", [P, I], F32)
-        z = tile("z", [P, 1], F32)
-        nc.scalar.activation(x[:], score[:], ACT.Exp, bias=neg_max[:], accum_out=z[:])
         x_pow = tile("x_pow", [P, I], F32)
-        nc.scalar.activation(x_pow[:], score[:], ACT.Exp, bias=neg_pmax[:], scale=power[:])
+        for h in range(HALVES):
+            col = slice(h, h + 1)
+            so_far = neg_max[:, h - 1 : h] if h else None
+            nc.vector.tensor_scalar(neg_score[:, slots(h)], score[h][:], -1.0, so_far, ALU.mult, ALU.min, accum_out=neg_max[:, col])
+            nc.scalar.activation(neg_pmax[:, col], neg_max[:, col], ACT.Copy, scale=power[:])
+            nc.scalar.activation(x[:, slots(h)], neg_score[:, slots(h)], ACT.Exp, bias=neg_max[:, col], scale=-1.0, accum_out=half_sum[:, col])
+            nc.scalar.activation(x_pow[:, slots(h)], score[h][:], ACT.Exp, bias=neg_pmax[:, col], scale=power[:])
 
-        vw_picked = gather("vw_picked", v_words, U16, "picked_words")
+        half_drop = tile("half_drop", [P, HALVES], F32)
+        nc.scalar.activation(half_drop[:], neg_max[:], ACT.Exp, bias=neg_max[:, 1:2], scale=-1.0)
+        z = tile("z", [P, 1], F32)
+        nc.scalar.activation(z[:], half_sum[:, 0:1], ACT.Identity, bias=half_sum[:, 1:2], scale=half_drop[:, 0:1])
+
+        vw_picked = tile("vw_picked", [P, I], U16, "picked_words")
+        gather_whole(vw_picked, v_words)
         page_sum = tile("page_sum", [P, G], F32)
         nc.vector.tensor_reduce(page_sum[:], paged(x[:]), AX.X, ALU.add)
-        vs_picked = gather("vs_picked", v_scales, U8, "picked_scales")
-        c0 = product("c0", g_codes, g_scales, vw_picked, vs_picked)
 
-        ln_z = tile("ln_z", [P, 1], F32)
-        nc.scalar.activation(ln_z[:], z[:], ACT.Ln)
-        neg_ln_z = tile("neg_ln_z", [P, 1], F32)
-        nc.gpsimd.tensor_scalar(neg_ln_z[:], ln_z[:], -1.0, 0.0, ALU.mult, ALU.add)
+        inv_z = tile("inv_z", [P, 1], F32)
+        nc.vector.reciprocal(inv_z[:], z[:])
+        weight = tile("weight", [P, HALVES], F32)
+        nc.gpsimd.tensor_scalar(weight[:], half_drop[:], inv_z[:], 0.0, ALU.mult, ALU.add)
+        p_weight = tile("p_weight", [P, HALVES], F32)
+        nc.gpsimd.tensor_scalar(p_weight[:], half_drop[:], inv_z[:], power[:], ALU.mult, ALU.mult)
+
         ln_s = tile("ln_s", [P, G], F32)
         nc.scalar.activation(ln_s[:], page_sum[:], ACT.Ln, bias=LN_FLOOR)
-        inv_z = tile("inv_z", [P, 1], F32)
-        nc.scalar.activation(inv_z[:], ln_z[:], ACT.Exp, scale=-1.0)
         share = tile("share", [P, G], F32)
-        nc.scalar.activation(share[:], ln_s[:], ACT.Exp, bias=neg_ln_z[:], scale=co_power[:])
+        nc.scalar.activation(share[:], ln_s[:], ACT.Exp, scale=co_power[:])
         norm = tile("norm", [P, G], F32)
-        nc.scalar.activation(norm[:], ln_s[:], ACT.Exp, bias=neg_ln_z[:], scale=neg_power[:])
+        nc.scalar.activation(norm[:], ln_s[:], ACT.Exp, scale=neg_power[:])
 
+        vs_picked = tile("vs_picked", [P, I], U8, "late_scales")
+        c0 = []
+        for h in range(HALVES):
+            gather_half(vs_picked, v_scales, h)
+            c0.append(product("c0", g_codes, g_scales, vw_picked, vs_picked, h))
         v = tile("v", [P, I], F32)
-        nc.vector.scalar_tensor_tensor(v[:], c0[:], 128.0, x_pow[:], ALU.mult, ALU.mult)
+        for h in range(HALVES):
+            nc.vector.scalar_tensor_tensor(v[:, slots(h)], c0[h][:], 128.0, x_pow[:, slots(h)], ALU.mult, ALU.mult)
         v_sum = tile("v_sum", [P, G], F32)
-        nc.vector.tensor_reduce(v_sum[:], paged(v[:]), AX.X, ALU.add)
-        row_terms = tile("row_terms", [P, G], F32)
-        row_total = tile("row_total", [P, 1], F32)
-        nc.vector.scalar_tensor_tensor(row_terms[:], v_sum[:], inv_z[:], share[:], ALU.mult, ALU.mult, accum_out=row_total[:])
+        for h in range(HALVES):
+            nc.vector.tensor_reduce(v_sum[:, pages(h)], paged(v[:, slots(h)]), AX.X, ALU.add)
+        w_sum = tile("w_sum", [P, G], F32)
+        by_half = "p (h g) -> p h g"
+        nc.vector.tensor_tensor(w_sum[:].rearrange(by_half, h=HALVES), v_sum[:].rearrange(by_half, h=HALVES), spread(weight[:], HALF_PAGES), ALU.mult)
+
+        row_terms = tile("row_terms", [P, HALVES, G], F32)
+        row_total = tile("row_total", [P, HALVES], F32)
+        for h in range(HALVES):
+            nc.vector.scalar_tensor_tensor(row_terms[:, h, :], w_sum[:], weight[:, h : h + 1], share[:], ALU.mult, ALU.mult, accum_out=row_total[:, h : h + 1])
         page_terms = tile("page_terms", [P, G], F32)
-        nc.vector.scalar_tensor_tensor(page_terms[:], v_sum[:], co_power[:], norm[:], ALU.mult, ALU.mult)
+        nc.vector.scalar_tensor_tensor(page_terms[:], w_sum[:], co_power[:], norm[:], ALU.mult, ALU.mult)
         direct = tile("direct", [P, I], F32)
-        nc.vector.scalar_tensor_tensor(paged(direct[:]), paged(v[:]), power[:], spread(share[:]), ALU.mult, ALU.mult)
         through = tile("through", [P, I], F32)
-        nc.vector.scalar_tensor_tensor(paged(through[:]), spread(page_terms[:]), row_total[:], paged(x[:]), ALU.subtract, ALU.mult)
+        for h in range(HALVES):
+            nc.vector.scalar_tensor_tensor(paged(direct[:, slots(h)]), paged(v[:, slots(h)]), p_weight[:, h : h + 1], spread(share[:, pages(h)], PAGE), ALU.mult, ALU.mult)
+        for h in range(HALVES):
+            nc.vector.scalar_tensor_tensor(paged(through[:, slots(h)]), spread(page_terms[:, pages(h)], PAGE), row_total[:, h : h + 1], paged(x[:, slots(h)]), ALU.subtract, ALU.mult)
 
         nc.vector.tensor_tensor(placed[:].indirect(offsets[:]), direct[:], through[:], ALU.add)
 
-        for c in range(T // OUT_CHUNK):
-            cols = slice(c * OUT_CHUNK, (c + 1) * OUT_CHUNK)
-            result = tile("result%d" % c, [P, OUT_CHUNK], F32)
+        start = 0
+        for c, width in enumerate(OUT_CHUNKS):
+            cols = slice(start, start + width)
+            start = start + width
+            result = tile("result%d" % c, [P, width], F32)
             nc.vector.tensor_tensor(result[:], placed[:, cols], old_sb[:, cols], ALU.add)
             queue = nc.sync if c % 2 == 0 else nc.scalar
             queue.dma_start(out=out[:, cols], in_=result[:])

@@ -49,19 +49,18 @@ def tile_attend_bsharedpower_s_kernel(tc, query, keys_words, keys_scales, pw, go
             return ap.unsqueeze(2).to_broadcast([P, ap.shape[1], times])
 
         offsets = tile("offsets", [P, I // 16], U16)
-        k_words = tile("k_words", [P, T], U16)
+        k_words = tile("k_words", [P, T], U16, "wide")
         v_words = tile("v_words", [P, T], U16)
         k_scales = tile("k_scales", [P, T], U8)
         v_scales = tile("v_scales", [P, T], U8)
         q_raw = tile("q_raw", [P, PACK, Q], F32)
         g_raw = tile("g_raw", [P, PACK, Q], F32)
         power = tile("power", [P, 1], F32)
-        old_sb = tile("old_sb", [P, T], F32)
         placed = tile("placed", [P, T], F32)
 
-        nc.gpsimd.memset(k_scales[:].bitcast(I32), 0)
-        nc.gpsimd.memset(v_scales[:].bitcast(I32), 0)
-        nc.gpsimd.memset(placed[:].bitcast(I32), 0)
+        nc.vector.memset(k_scales[:].bitcast(I32), 0)
+        nc.vector.memset(v_scales[:].bitcast(I32), 0)
+        nc.vector.memset(placed[:].bitcast(I32), 0)
 
         def load_scales(queue, dst, src, quads):
             for quad in quads:
@@ -76,13 +75,12 @@ def tile_attend_bsharedpower_s_kernel(tc, query, keys_words, keys_scales, pw, go
         nc.sync.dma_start(out=g_raw[:], in_=gout.rearrange("(p j) w -> p j w", j=PACK))
         nc.sync.dma_start(out=v_words[:].bitcast(I32), in_=vals_words[0].bitcast(I32))
         load_scales(nc.sync, v_scales, vals_scales, range(4))
-        nc.sync.dma_start(out=old_sb[:], in_=old)
 
         def gather_whole(picked, window):
             nc.vector.tensor_copy(picked[:], window[:].indirect(offsets[:]))
 
         def gather_half(picked, window, h):
-            nc.vector.tensor_copy(picked[:, slots(h)], window[:].indirect(offsets[:, h * HALF // 16 : (h + 1) * HALF // 16]))
+            nc.vector.tensor_copy(picked, window[:].indirect(offsets[:, h * HALF // 16 : (h + 1) * HALF // 16]))
 
         def quantize(name, raw):
             grouped = tile(name + "_grouped", [P, Q, PACK], BF16)
@@ -99,31 +97,33 @@ def tile_attend_bsharedpower_s_kernel(tc, query, keys_words, keys_scales, pw, go
                 lhsT=codes[:].bitcast(FP8X4),
                 lhsT_scale=scales[:],
                 rhs=words[:, slots(h)].bitcast(FP4X4),
-                rhs_scale=word_scales[:, slots(h)],
+                rhs_scale=word_scales,
                 start=True,
                 stop=True,
             )
             return acc
 
-        ks_picked = tile("ks_picked", [P, I], U8)
+        ks_picked = tile("ks_picked", [P, I], U8, "early_scales")
         kw_picked = tile("kw_picked", [P, I], U16, "picked_words")
         gather_whole(ks_picked, k_scales)
         q_codes, q_scales = quantize("q", q_raw)
         score = []
         for h in range(HALVES):
-            gather_half(kw_picked, k_words, h)
-            score.append(product("score", q_codes, q_scales, kw_picked, ks_picked, h))
+            gather_half(kw_picked[:, slots(h)], k_words, h)
+            score.append(product("score", q_codes, q_scales, kw_picked, ks_picked[:, slots(h)], h))
         g_codes, g_scales = quantize("g", g_raw)
+        old_sb = tile("old_sb", [P, T], F32, "wide")
+        nc.sync.dma_start(out=old_sb[:], in_=old)
 
         neg_power = tile("neg_power", [P, 1], F32)
         co_power = tile("co_power", [P, 1], F32)
-        nc.gpsimd.tensor_scalar(neg_power[:], power[:], -1.0, 0.0, ALU.mult, ALU.add)
-        nc.gpsimd.tensor_scalar(co_power[:], power[:], -1.0, 1.0, ALU.mult, ALU.add)
+        nc.scalar.activation(neg_power[:], power[:], ACT.Copy, scale=-1.0)
+        nc.scalar.activation(co_power[:], power[:], ACT.Copy, scale=-1.0, bias=1.0)
 
         neg_score = tile("neg_score", [P, I], F32)
         neg_max = tile("neg_max", [P, HALVES], F32)
-        neg_pmax = tile("neg_pmax", [P, HALVES], F32, "late_scales")
-        half_sum = tile("half_sum", [P, HALVES], F32)
+        neg_pmax = tile("neg_pmax", [P, HALVES], F32)
+        half_sum = tile("half_sum", [P, HALVES], F32, "sums")
         x = tile("x", [P, I], F32)
         x_pow = tile("x_pow", [P, I], F32)
         for h in range(HALVES):
@@ -136,20 +136,28 @@ def tile_attend_bsharedpower_s_kernel(tc, query, keys_words, keys_scales, pw, go
 
         half_drop = tile("half_drop", [P, HALVES], F32)
         nc.scalar.activation(half_drop[:], neg_max[:], ACT.Exp, bias=neg_max[:, 1:2], scale=-1.0)
-        z = tile("z", [P, 1], F32)
+        z = tile("z", [P, 1], F32, "late_scales")
         nc.scalar.activation(z[:], half_sum[:, 0:1], ACT.Identity, bias=half_sum[:, 1:2], scale=half_drop[:, 0:1])
 
         vw_picked = tile("vw_picked", [P, I], U16, "picked_words")
         gather_whole(vw_picked, v_words)
-        page_sum = tile("page_sum", [P, G], F32)
-        nc.vector.tensor_reduce(page_sum[:], paged(x[:]), AX.X, ALU.add)
+        c0 = []
 
+        def values_half(h, tag):
+            vs_picked = tile("vs_picked%d" % h, [P, HALF], U8, tag)
+            gather_half(vs_picked[:], v_scales, h)
+            c0.append(product("c0", g_codes, g_scales, vw_picked, vs_picked[:], h))
+
+        values_half(0, "early_scales")
         inv_z = tile("inv_z", [P, 1], F32)
         nc.vector.reciprocal(inv_z[:], z[:])
+        page_sum = tile("page_sum", [P, G], F32, "sums")
+        nc.vector.tensor_reduce(page_sum[:], paged(x[:]), AX.X, ALU.add)
+
+        out_weight = tile("out_weight", [P, HALVES], F32)
+        nc.vector.tensor_scalar(out_weight[:], half_drop[:], inv_z[:], 128.0, ALU.mult, ALU.mult)
         weight = tile("weight", [P, HALVES], F32)
-        nc.gpsimd.tensor_scalar(weight[:], half_drop[:], inv_z[:], 0.0, ALU.mult, ALU.add)
-        p_weight = tile("p_weight", [P, HALVES], F32)
-        nc.gpsimd.tensor_scalar(p_weight[:], half_drop[:], inv_z[:], power[:], ALU.mult, ALU.mult)
+        nc.vector.tensor_scalar(weight[:], half_drop[:], inv_z[:], None, ALU.mult)
 
         ln_s = tile("ln_s", [P, G], F32)
         nc.scalar.activation(ln_s[:], page_sum[:], ACT.Ln, bias=LN_FLOOR)
@@ -158,31 +166,22 @@ def tile_attend_bsharedpower_s_kernel(tc, query, keys_words, keys_scales, pw, go
         norm = tile("norm", [P, G], F32)
         nc.scalar.activation(norm[:], ln_s[:], ACT.Exp, scale=neg_power[:])
 
-        vs_picked = tile("vs_picked", [P, I], U8, "late_scales")
-        c0 = []
-        for h in range(HALVES):
-            gather_half(vs_picked, v_scales, h)
-            c0.append(product("c0", g_codes, g_scales, vw_picked, vs_picked, h))
+        values_half(1, "late_scales")
         v = tile("v", [P, I], F32)
-        for h in range(HALVES):
-            nc.vector.scalar_tensor_tensor(v[:, slots(h)], c0[h][:], 128.0, x_pow[:, slots(h)], ALU.mult, ALU.mult)
         v_sum = tile("v_sum", [P, G], F32)
         for h in range(HALVES):
+            nc.vector.scalar_tensor_tensor(v[:, slots(h)], c0[h][:], out_weight[:, h : h + 1], x_pow[:, slots(h)], ALU.mult, ALU.mult)
             nc.vector.tensor_reduce(v_sum[:, pages(h)], paged(v[:, slots(h)]), AX.X, ALU.add)
-        w_sum = tile("w_sum", [P, G], F32)
-        by_half = "p (h g) -> p h g"
-        nc.vector.tensor_tensor(w_sum[:].rearrange(by_half, h=HALVES), v_sum[:].rearrange(by_half, h=HALVES), spread(weight[:], HALF_PAGES), ALU.mult)
 
         row_terms = tile("row_terms", [P, HALVES, G], F32)
         row_total = tile("row_total", [P, HALVES], F32)
         for h in range(HALVES):
-            nc.vector.scalar_tensor_tensor(row_terms[:, h, :], w_sum[:], weight[:, h : h + 1], share[:], ALU.mult, ALU.mult, accum_out=row_total[:, h : h + 1])
+            nc.vector.scalar_tensor_tensor(row_terms[:, h, :], v_sum[:], weight[:, h : h + 1], share[:], ALU.mult, ALU.mult, accum_out=row_total[:, h : h + 1])
         page_terms = tile("page_terms", [P, G], F32)
-        nc.vector.scalar_tensor_tensor(page_terms[:], w_sum[:], co_power[:], norm[:], ALU.mult, ALU.mult)
+        nc.vector.scalar_tensor_tensor(page_terms[:], v_sum[:], co_power[:], norm[:], ALU.mult, ALU.mult)
         direct = tile("direct", [P, I], F32)
         through = tile("through", [P, I], F32)
-        for h in range(HALVES):
-            nc.vector.scalar_tensor_tensor(paged(direct[:, slots(h)]), paged(v[:, slots(h)]), p_weight[:, h : h + 1], spread(share[:, pages(h)], PAGE), ALU.mult, ALU.mult)
+        nc.vector.scalar_tensor_tensor(paged(direct[:]), paged(v[:]), power[:], spread(share[:], PAGE), ALU.mult, ALU.mult)
         for h in range(HALVES):
             nc.vector.scalar_tensor_tensor(paged(through[:, slots(h)]), spread(page_terms[:, pages(h)], PAGE), row_total[:, h : h + 1], paged(x[:, slots(h)]), ALU.subtract, ALU.mult)
 

from contextlib import ExitStack

import concourse.mybir as mybir

D, E, T, I, Q, G = 512, 512, 2048, 512, 128, 64
PAGE = I // G
P = 128
PACK = 4
FLOPS = 2 * Q * I * (D + E)

F32 = mybir.dt.float32
BF16 = mybir.dt.bfloat16
I32 = mybir.dt.int32
U32 = mybir.dt.uint32
U16 = mybir.dt.uint16
U8 = mybir.dt.uint8
FP8X4 = mybir.dt.float8_e4m3fn_x4
FP4X4 = mybir.dt.float4_e2m1fn_x4
ALU = mybir.AluOpType
ACT = mybir.ActivationFunctionType
AX = mybir.AxisListType

HALVES = 2
HALF = I // HALVES
HALF_PAGES = G // HALVES
OUT_CHUNKS = (256, 512, 512, 512, 256)
LN_FLOOR = 2.0 ** -62


def tile_attend_bsharedpower_s_kernel(tc, query, keys_words, keys_scales, pw, gout, vals_words, vals_scales, old, offs, out):
    nc = tc.nc
    with ExitStack() as ctx:
        sb = ctx.enter_context(tc.tile_pool(name="sb", bufs=1))
        ps = ctx.enter_context(tc.psum_pool(name="ps", bufs=1))

        def tile(name, shape, dtype, tag=""):
            return sb.tile(shape, dtype, name=name, tag=tag or name, align_bytes=64)

        def slots(h):
            return slice(h * HALF, (h + 1) * HALF)

        def pages(h):
            return slice(h * HALF_PAGES, (h + 1) * HALF_PAGES)

        def paged(ap):
            return ap.rearrange("p (g j) -> p g j", j=PAGE)

        def spread(ap, times):
            return ap.unsqueeze(2).to_broadcast([P, ap.shape[1], times])

        offsets = tile("offsets", [P, I // 16], U16)
        k_words = tile("k_words", [P, T], U16, "wide")
        v_words = tile("v_words", [P, T], U16)
        k_scales = tile("k_scales", [P, T], U8)
        v_scales = tile("v_scales", [P, T], U8)
        q_raw = tile("q_raw", [P, PACK, Q], F32)
        g_raw = tile("g_raw", [P, PACK, Q], F32)
        power = tile("power", [P, 1], F32)
        placed = tile("placed", [P, T], F32)

        nc.vector.memset(k_scales[:].bitcast(I32), 0)
        nc.vector.memset(v_scales[:].bitcast(I32), 0)
        nc.vector.memset(placed[:].bitcast(I32), 0)

        def load_scales(queue, dst, src, quads):
            for quad in quads:
                queue.dma_start(out=dst[32 * quad : 32 * quad + 4, :].bitcast(I32), in_=src[0, 4 * quad : 4 * quad + 4, :].bitcast(I32))

        nc.sync.dma_start(offsets[:], offs)
        nc.sync.dma_start(out=q_raw[:], in_=query.rearrange("(p j) w -> p j w", j=PACK))
        nc.scalar.dma_start(out=power[:], in_=pw)
        load_scales(nc.sync, k_scales, keys_scales, (0, 1))
        load_scales(nc.scalar, k_scales, keys_scales, (2, 3))
        nc.sync.dma_start(out=k_words[:].bitcast(I32), in_=keys_words[0].bitcast(I32))
        nc.sync.dma_start(out=g_raw[:], in_=gout.rearrange("(p j) w -> p j w", j=PACK))
        nc.sync.dma_start(out=v_words[:].bitcast(I32), in_=vals_words[0].bitcast(I32))
        load_scales(nc.sync, v_scales, vals_scales, range(4))

        def gather_whole(picked, window):
            nc.vector.tensor_copy(picked[:], window[:].indirect(offsets[:]))

        def gather_half(picked, window, h):
            nc.vector.tensor_copy(picked, window[:].indirect(offsets[:, h * HALF // 16 : (h + 1) * HALF // 16]))

        def quantize(name, raw):
            grouped = tile(name + "_grouped", [P, Q, PACK], BF16)
            nc.scalar.copy(out=grouped[:], in_=raw[:].rearrange("p j w -> p w j"))
            codes = tile(name + "_codes", [P, Q], U32)
            scales = tile(name + "_scales", [P, Q], U8)
            nc.vector.quantize_mx(out=codes[:].bitcast(FP8X4), scales=scales[:], in_=grouped[:].rearrange("p w j -> p (w j)"))
            return codes, scales

        def product(name, codes, scales, words, word_scales, h):
            acc = ps.tile([P, HALF], F32, name="%s%d" % (name, h))
            nc.tensor.matmul_mx(
                out=acc[:],
                lhsT=codes[:].bitcast(FP8X4),
                lhsT_scale=scales[:],
                rhs=words[:, slots(h)].bitcast(FP4X4),
                rhs_scale=word_scales,
                start=True,
                stop=True,
            )
            return acc

        ks_picked = tile("ks_picked", [P, I], U8, "early_scales")
        kw_picked = tile("kw_picked", [P, I], U16, "picked_words")
        gather_whole(ks_picked, k_scales)
        q_codes, q_scales = quantize("q", q_raw)
        score = []
        for h in range(HALVES):
            gather_half(kw_picked[:, slots(h)], k_words, h)
            score.append(product("score", q_codes, q_scales, kw_picked, ks_picked[:, slots(h)], h))
        g_codes, g_scales = quantize("g", g_raw)
        old_sb = tile("old_sb", [P, T], F32, "wide")
        nc.sync.dma_start(out=old_sb[:], in_=old)

        neg_power = tile("neg_power", [P, 1], F32)
        co_power = tile("co_power", [P, 1], F32)
        nc.scalar.activation(neg_power[:], power[:], ACT.Copy, scale=-1.0)
        nc.scalar.activation(co_power[:], power[:], ACT.Copy, scale=-1.0, bias=1.0)

        neg_score = tile("neg_score", [P, I], F32)
        neg_max = tile("neg_max", [P, HALVES], F32)
        neg_pmax = tile("neg_pmax", [P, HALVES], F32)
        half_sum = tile("half_sum", [P, HALVES], F32, "sums")
        x = tile("x", [P, I], F32)
        x_pow = tile("x_pow", [P, I], F32)
        for h in range(HALVES):
            col = slice(h, h + 1)
            so_far = neg_max[:, h - 1 : h] if h else None
            nc.vector.tensor_scalar(neg_score[:, slots(h)], score[h][:], -1.0, so_far, ALU.mult, ALU.min, accum_out=neg_max[:, col])
            nc.scalar.activation(neg_pmax[:, col], neg_max[:, col], ACT.Copy, scale=power[:])
            nc.scalar.activation(x[:, slots(h)], neg_score[:, slots(h)], ACT.Exp, bias=neg_max[:, col], scale=-1.0, accum_out=half_sum[:, col])
            nc.scalar.activation(x_pow[:, slots(h)], score[h][:], ACT.Exp, bias=neg_pmax[:, col], scale=power[:])

        half_drop = tile("half_drop", [P, HALVES], F32)
        nc.scalar.activation(half_drop[:], neg_max[:], ACT.Exp, bias=neg_max[:, 1:2], scale=-1.0)
        z = tile("z", [P, 1], F32, "late_scales")
        nc.scalar.activation(z[:], half_sum[:, 0:1], ACT.Identity, bias=half_sum[:, 1:2], scale=half_drop[:, 0:1])

        vw_picked = tile("vw_picked", [P, I], U16, "picked_words")
        gather_whole(vw_picked, v_words)
        c0 = []

        def values_half(h, tag):
            vs_picked = tile("vs_picked%d" % h, [P, HALF], U8, tag)
            gather_half(vs_picked[:], v_scales, h)
            c0.append(product("c0", g_codes, g_scales, vw_picked, vs_picked[:], h))

        values_half(0, "early_scales")
        inv_z = tile("inv_z", [P, 1], F32)
        nc.vector.reciprocal(inv_z[:], z[:])
        page_sum = tile("page_sum", [P, G], F32, "sums")
        nc.vector.tensor_reduce(page_sum[:], paged(x[:]), AX.X, ALU.add)

        out_weight = tile("out_weight", [P, HALVES], F32)
        nc.vector.tensor_scalar(out_weight[:], half_drop[:], inv_z[:], 128.0, ALU.mult, ALU.mult)
        weight = tile("weight", [P, HALVES], F32)
        nc.vector.tensor_scalar(weight[:], half_drop[:], inv_z[:], None, ALU.mult)

        ln_s = tile("ln_s", [P, G], F32)
        nc.scalar.activation(ln_s[:], page_sum[:], ACT.Ln, bias=LN_FLOOR)
        share = tile("share", [P, G], F32)
        nc.scalar.activation(share[:], ln_s[:], ACT.Exp, scale=co_power[:])
        norm = tile("norm", [P, G], F32)
        nc.scalar.activation(norm[:], ln_s[:], ACT.Exp, scale=neg_power[:])

        values_half(1, "late_scales")
        v = tile("v", [P, I], F32)
        v_sum = tile("v_sum", [P, G], F32)
        for h in range(HALVES):
            nc.vector.scalar_tensor_tensor(v[:, slots(h)], c0[h][:], out_weight[:, h : h + 1], x_pow[:, slots(h)], ALU.mult, ALU.mult)
            nc.vector.tensor_reduce(v_sum[:, pages(h)], paged(v[:, slots(h)]), AX.X, ALU.add)

        row_terms = tile("row_terms", [P, HALVES, G], F32)
        row_total = tile("row_total", [P, HALVES], F32)
        for h in range(HALVES):
            nc.vector.scalar_tensor_tensor(row_terms[:, h, :], v_sum[:], weight[:, h : h + 1], share[:], ALU.mult, ALU.mult, accum_out=row_total[:, h : h + 1])
        page_terms = tile("page_terms", [P, G], F32)
        nc.vector.scalar_tensor_tensor(page_terms[:], v_sum[:], co_power[:], norm[:], ALU.mult, ALU.mult)
        direct = tile("direct", [P, I], F32)
        through = tile("through", [P, I], F32)
        nc.vector.scalar_tensor_tensor(paged(direct[:]), paged(v[:]), power[:], spread(share[:], PAGE), ALU.mult, ALU.mult)
        for h in range(HALVES):
            nc.vector.scalar_tensor_tensor(paged(through[:, slots(h)]), spread(page_terms[:, pages(h)], PAGE), row_total[:, h : h + 1], paged(x[:, slots(h)]), ALU.subtract, ALU.mult)

        nc.vector.tensor_tensor(placed[:].indirect(offsets[:]), direct[:], through[:], ALU.add)

        start = 0
        for c, width in enumerate(OUT_CHUNKS):
            cols = slice(start, start + width)
            start = start + width
            result = tile("result%d" % c, [P, width], F32)
            nc.vector.tensor_tensor(result[:], placed[:, cols], old_sb[:, cols], ALU.add)
            queue = nc.sync if c % 2 == 0 else nc.scalar
            queue.dma_start(out=out[:, cols], in_=result[:])
